import numpy as np
import ml_dtypes


def mxq(x, axis, fmt="e4m3"):
    dtype, down = {"e4m3": (ml_dtypes.float8_e4m3fn, 7), "e5m2": (ml_dtypes.float8_e5m2, 14)}[fmt]
    v = np.moveaxis(np.asarray(x, np.float32).astype(ml_dtypes.bfloat16).astype(np.float64), axis, -1)
    blocks = v.reshape(v.shape[:-1] + (-1, 32))
    amax = np.abs(blocks).max(-1, keepdims=True)
    byte = np.maximum(np.where(amax > 0, np.frexp(amax)[1] - 1 + 127, 0) - down, 1)
    scale = np.exp2(byte - 127.0)
    codes = (blocks / scale).astype(np.float32).astype(dtype).astype(np.float64)
    return np.moveaxis((codes * scale).reshape(v.shape), -1, axis)


WIDE = False


def mx_kscale(k):
    if not WIDE:
        return np.ones(k)
    levels = np.array([10, -10, 5, -5, 0])
    if k % 512:
        return np.exp2(np.random.permutation(np.resize(levels, k // 32))).repeat(32)
    a = np.empty((k // 512, 16))
    for p in range(k // 512):
        a[p, :8] = np.random.permutation(np.resize(levels, 8))
        for g in range(8):
            far = levels[np.abs(levels - a[p, g]) >= 10]
            a[p, g + 8] = far[np.random.randint(len(far))]
    return np.exp2(a.ravel()).repeat(32)


def f64(x):
    return np.asarray(x).astype(np.float64)


def striped(idx):
    return np.tile(idx.reshape(-1, 16).T, (8, 1)).astype(np.uint16)


def unstriped(offs):
    return offs[:16].T.reshape(-1).astype(np.int64)


def striped8(idx):
    return np.concatenate([x.reshape(-1, 16).T for x in idx]).astype(np.uint16)


def runs(offs, k):
    lists = np.stack([offs[16 * r : 16 * r + 16].T.reshape(-1) for r in range(8)]).astype(np.int64)
    return lists[np.arange(k) % 512 // 64]


def pack_weight(w):
    k, n = w.shape
    w = f64(np.asarray(w, np.float32).astype(ml_dtypes.bfloat16)).reshape(k // 32, 32, n)
    amax = np.abs(w).max(1)
    byte = np.clip(np.where(amax > 0, np.frexp(amax)[1] - 1 + 127 - 7, 1), 1, 254)
    scaled = (w * np.exp2(127.0 - byte)[:, None, :]).reshape(k, n).astype(np.float32)
    words = np.ascontiguousarray(scaled.reshape(k // 512, 128, 4, n).transpose(0, 1, 3, 2)).astype(ml_dtypes.float8_e4m3fn).view(np.uint8)
    return words, np.ascontiguousarray(byte.astype(np.uint8).reshape(k // 512, 16, n))


def unpack_weight(words, scales):
    g, p, n, _ = words.shape
    vals = np.ascontiguousarray(words).view(ml_dtypes.float8_e4m3fn).astype(np.float64) * np.repeat(np.exp2(scales.astype(np.float64) - 127.0), 8, axis=1)[..., None]
    return vals.transpose(0, 1, 3, 2).reshape(g * 512, n)


def sigmoid(v):
    return 1.0 / (1.0 + np.exp(-np.maximum(v, -700.0)))


K, T, S, N, H, J, W = 512, 2048, 512, 512, 512, 512, 256


def setup_inputs():
    n = np.random.standard_normal
    s = mx_kscale(K)[:, None]
    u = mx_kscale(H)
    packed_xT = pack_weight(n((K, T)) * s)
    perm = np.stack([np.random.permutation(S) for _ in range(8)])
    return {
        "x_words": packed_xT[0],
        "x_scales": packed_xT[1],
        "w1": (n((K, H)) / np.sqrt(K) / s).astype(np.float32),
        "tab": n((H, J)).astype(np.float32),
        "gn": (np.random.uniform(0.5, 1.5, (H, 1)) * u[:, None]).astype(np.float32),
        "w2": (n((H, N)) / np.sqrt(H) / u[:, None]).astype(np.float32),
        "gm": (np.random.uniform(0.5, 1.5, (H, 1)) * u[:, None]).astype(np.float32),
        "w3": (n((H, N)) / np.sqrt(H) / u[:, None]).astype(np.float32),
        "offs": striped(np.random.permutation(T)[:S]),
        "n1": striped8(np.random.randint(0, J, (8, S))),
        "n2": striped8(np.random.randint(0, J, (8, S))),
        "n3": striped8(np.stack([np.random.permutation(S) for _ in range(8)])),
        "n4": striped8(perm[:, :W]),
        "n5": striped8(perm[:, W:]),
        "n6": striped8(np.stack([np.random.permutation(S) for _ in range(8)])),
        "n7": striped8(np.stack([np.random.permutation(S) for _ in range(8)])),
    }


def reference(x_words, x_scales, w1, tab, gn, w2, gm, w3, offs, n1, n2, n3, n4, n5, n6, n7):
    xq = unpack_weight(x_words, x_scales)[:, unstriped(offs)]
    y = mxq(f64(w1), 0, "e4m3").T @ xq
    z = f64(gn) * ((y[np.arange(H)[:, None], runs(n3, H)]) * (f64(tab)[np.arange(H)[:, None], runs(n1, H)]) + f64(tab)[np.arange(H)[:, None], runs(n2, H)])
    a = mxq(f64(w2), 0, "e4m3").T @ mxq(z, 0, "e4m3")
    pa = y[np.arange(H)[:, None], runs(n4, H)]
    pb = y[np.arange(H)[:, None], runs(n5, H)]
    ra = pa * sigmoid(pb)
    ds = y.copy()
    ds[np.arange(H)[:, None], runs(n5, H)] = ra
    z2 = f64(gm) * ds
    b = mxq(f64(w3), 0, "e4m3").T @ mxq(z2, 0, "e4m3")
    return (a + a[np.arange(N)[:, None], runs(n6, N)]) * (sigmoid(b + b[np.arange(N)[:, None], runs(n7, N)]))

@@ -1,0 +1,261 @@
+from contextlib import ExitStack
+
+import concourse.mybir as mybir
+from concourse.masks import make_identity
+
+K, T, S, N, H = 512, 2048, 512, 512, 512
+FLOPS = 3 * 2 * 512 * 512 * 512
+
+F32 = mybir.dt.float32
+BF16 = mybir.dt.bfloat16
+I32 = mybir.dt.int32
+U32 = mybir.dt.uint32
+U16 = mybir.dt.uint16
+U8 = mybir.dt.uint8
+FP8X4 = mybir.dt.float8_e4m3fn_x4
+ACT = mybir.ActivationFunctionType
+ALU = mybir.AluOpType
+
+P = 128
+PACK = 4
+HALF = S // 2
+
+
+def tile_picked_forktriebkindafold_none_p_kernel(
+    tc, x_words, x_scales, w1, tab, gn, w2, gm, w3, offs, n1, n2, n3, n4, n5, n6, n7, out
+):
+    nc = tc.nc
+    planes = range(PACK)
+    halves = [slice(0, HALF), slice(HALF, S)]
+
+    with ExitStack() as ctx:
+        keep = ctx.enter_context(tc.tile_pool(name="keep", bufs=1))
+        psum = ctx.enter_context(tc.psum_pool(name="psum", bufs=1))
+
+        def sb(name, shape, dtype):
+            return keep.tile(shape, dtype, name=name, align_bytes=64)
+
+        def load_list(name, src):
+            tile = keep.tile(list(src.shape), U16, name=name)
+            nc.sync.dma_start(tile[:], src)
+            return tile
+
+        def load_weight(name, w):
+            raw = sb(name + "_raw", [P, PACK, N], F32)
+            nc.sync.dma_start(out=raw[:], in_=w.rearrange("(p j) c -> p j c", j=PACK))
+            return raw
+
+        def gather(engine, dst, window, lst, cols, func=ACT.Copy):
+            picked = window[:].indirect(lst[:, cols.start // 16 : cols.stop // 16])
+            if engine is nc.vector:
+                nc.vector.tensor_copy(out=dst, in_=picked)
+            else:
+                nc.scalar.activation(out=dst, in_=picked, func=func)
+
+        def copy(engine, dst, src):
+            if engine is nc.vector:
+                nc.vector.tensor_copy(out=dst, in_=src)
+            else:
+                nc.scalar.copy(out=dst, in_=src)
+
+        def deal_weight(engine, name, raw):
+            dealt = sb(name + "_bf", [P, N * PACK], BF16)
+            copy(
+                engine,
+                dealt[:].rearrange("p (t m j) -> p m j t", t=PACK, j=PACK),
+                raw[:].rearrange("p j (m t) -> p m j t", t=PACK),
+            )
+            return dealt
+
+        def quantize(name, values, parts):
+            codes = sb(name + "_codes", [P, S], U32)
+            scales = sb(name + "_scales", [P, S], U8)
+            for cols in parts:
+                nc.vector.quantize_mx(
+                    out=codes[:, cols].bitcast(FP8X4),
+                    scales=scales[:, cols],
+                    in_=values[:, PACK * cols.start : PACK * cols.stop],
+                )
+            return codes, scales
+
+        def weave(engine, name, rows):
+            woven = sb(name, [P, S * PACK], BF16)
+            for cols in halves:
+                copy(
+                    engine,
+                    woven[:, PACK * cols.start : PACK * cols.stop].rearrange("p (c i t) -> p c t i", i=4, t=PACK),
+                    rows[:, :, cols].rearrange("p t (c i) -> p c t i", i=4),
+                )
+            return woven
+
+        def product(tag, weight, moving):
+            banks = []
+            for t in planes:
+                bank = psum.tile([P, S], F32, name=f"{tag}{t}", tag=f"{tag}{t}")
+                m_cols = slice(P * t, P * (t + 1))
+                nc.tensor.matmul_mx(
+                    out=bank[:],
+                    lhsT=weight[0][:, m_cols].bitcast(FP8X4),
+                    lhsT_scale=weight[1][:, m_cols],
+                    rhs=moving[0][:].bitcast(FP8X4),
+                    rhs_scale=moving[1][:],
+                    start=True,
+                    stop=True,
+                )
+                banks.append(bank)
+            return banks
+
+        x_scale_rows = sb("x_scale_rows", [P, T], U8)
+        nc.vector.memset(x_scale_rows[:].bitcast(I32), 0)
+        gn_sb = sb("gn_sb", [P, PACK], F32)
+        gm_sb = sb("gm_sb", [P, PACK], F32)
+        ident = sb("ident", [P, P], F32)
+        make_identity(nc, ident[:])
+
+        tab_rows = tab.rearrange("(p t) c -> p t c", t=PACK)
+        tab_sb = [sb(f"tab{t}", [P, S], F32) for t in planes]
+        n1_sb = load_list("n1_sb", n1)
+        nc.sync.dma_start(out=tab_sb[0][:], in_=tab_rows[:, 0, :])
+        n2_sb = load_list("n2_sb", n2)
+        nc.sync.dma_start(out=tab_sb[1][:], in_=tab_rows[:, 1, :])
+        for q in range(4):
+            nc.sync.dma_start(
+                out=x_scale_rows[32 * q : 32 * q + 4, :].bitcast(I32),
+                in_=x_scales[0, 4 * q : 4 * q + 4, :].bitcast(I32),
+            )
+        for t in range(2, PACK):
+            nc.sync.dma_start(out=tab_sb[t][:], in_=tab_rows[:, t, :])
+        offs_sb = load_list("offs_sb", offs)
+        w1_raw = load_weight("w1", w1)
+        x_word_rows = sb("x_word_rows", [P, T], I32)
+        nc.sync.dma_start(out=x_word_rows[:], in_=x_words[0].rearrange("p n t -> p (n t)").bitcast(I32))
+        n3_sb = load_list("n3_sb", n3)
+        nc.sync.dma_start(out=gn_sb[:], in_=gn.rearrange("(p t) o -> p (t o)", t=PACK))
+        w2_raw = load_weight("w2", w2)
+        n5_sb = load_list("n5_sb", n5)
+        n4_sb = load_list("n4_sb", n4)
+        w3_raw = load_weight("w3", w3)
+        nc.sync.dma_start(out=gm_sb[:], in_=gm.rearrange("(p t) o -> p (t o)", t=PACK))
+        n6_sb = load_list("n6_sb", n6)
+        n7_sb = load_list("n7_sb", n7)
+
+        factor = [sb(f"factor{t}", [P, S], F32) for t in planes]
+        shift = [sb(f"shift{t}", [P, S], F32) for t in planes]
+        for t in planes:
+            for cols in halves:
+                gather(nc.scalar, factor[t][:, cols], tab_sb[t], n1_sb, cols)
+            for cols in halves:
+                gather(nc.vector if t < 2 else nc.scalar, shift[t][:, cols], tab_sb[t], n2_sb, cols)
+
+        x_codes = sb("x_codes", [P, S], U32)
+        x_scale = sb("x_scale", [P, S], U8)
+        nc.vector.tensor_copy(out=x_scale[:], in_=x_scale_rows[:].indirect(offs_sb[:]))
+        w1_q = quantize("w1", deal_weight(nc.vector, "w1", w1_raw), [slice(0, S)])
+        nc.vector.tensor_copy(out=x_codes[:], in_=x_word_rows[:].bitcast(U32).indirect(offs_sb[:]))
+        y_ps = product("lo", w1_q, (x_codes, x_scale))
+
+        y_sb = [sb(f"y{t}", [P, S], F32) for t in planes]
+        y_at = [sb(f"y_at{t}", [P, S], F32) for t in planes]
+        scaled = [sb(f"scaled{t}", [P, S], F32) for t in planes]
+        z_rows = sb("z_rows", [P, PACK, S], BF16)
+        w2_q = quantize("w2", deal_weight(nc.vector, "w2", w2_raw), [slice(0, S)])
+
+        def scale_up(t, cols):
+            nc.vector.scalar_tensor_tensor(
+                out=scaled[t][:, cols], in0=y_at[t][:, cols], scalar=gn_sb[:, t : t + 1], in1=factor[t][:, cols],
+                op0=ALU.mult, op1=ALU.mult,
+            )
+
+        def add_shift(t, cols):
+            nc.vector.scalar_tensor_tensor(
+                out=z_rows[:, t, cols], in0=shift[t][:, cols], scalar=gn_sb[:, t : t + 1], in1=scaled[t][:, cols],
+                op0=ALU.mult, op1=ALU.add,
+            )
+
+        last = PACK - 1
+        every = slice(0, S)
+        nc.scalar.copy(out=y_sb[0][:], in_=y_ps[0][:])
+        for t in planes:
+            if t < last:
+                nc.scalar.copy(out=y_sb[t + 1][:], in_=y_ps[t + 1][:])
+            for cols in halves:
+                gather(nc.scalar, y_at[t][:, cols], y_sb[t], n3_sb, cols)
+            if t < last:
+                scale_up(t, every)
+            if t > 0:
+                add_shift(t - 1, every)
+            if t == 0:
+                w3_q = quantize("w3", deal_weight(nc.vector, "w3", w3_raw), [every])
+        for cols in halves:
+            scale_up(last, cols)
+        for cols in halves:
+            add_shift(last, cols)
+        z_q = quantize("z", weave(nc.vector, "z_bf", z_rows), halves)
+        a_ps = product("hi", w2_q, z_q)
+
+        whole = slice(0, HALF)
+        gate = [sb(f"gate{t}", [P, HALF], F32) for t in planes]
+        kept = [sb(f"kept{t}", [P, HALF], F32) for t in planes]
+        z2_rows = sb("z2_rows", [P, PACK, S], BF16)
+        for t in planes:
+            gather(nc.scalar, gate[t][:], y_sb[t], n5_sb, whole, func=ACT.Sigmoid)
+            gather(nc.scalar, kept[t][:], y_sb[t], n4_sb, whole)
+        for t in planes:
+            nc.vector.tensor_tensor(out=y_sb[t][:].indirect(n5_sb[:]), in0=kept[t][:], in1=gate[t][:], op=ALU.mult)
+            if t > 0:
+                nc.vector.tensor_scalar(
+                    out=z2_rows[:, t - 1, :], in0=y_sb[t - 1][:], scalar1=gm_sb[:, t - 1 : t], scalar2=None, op0=ALU.mult
+                )
+
+        a_sb = [sb(f"a{t}", [P, S], F32) for t in planes]
+        a_at = [sb(f"a_at{t}", [P, S], F32) for t in planes]
+        a_sum = [sb(f"a_sum{t}", [P, S], F32) for t in planes]
+        nc.scalar.copy(out=a_sb[0][:], in_=a_ps[0][:])
+        for t in planes:
+            if t < last:
+                nc.scalar.copy(out=a_sb[t + 1][:], in_=a_ps[t + 1][:])
+            for cols in halves:
+                gather(nc.scalar, a_at[t][:, cols], a_sb[t], n6_sb, cols)
+        for cols in halves:
+            nc.vector.tensor_scalar(
+                out=z2_rows[:, last, cols], in0=y_sb[last][:, cols], scalar1=gm_sb[:, last:], scalar2=None, op0=ALU.mult
+            )
+        z2_q = quantize("z2", weave(nc.vector, "z2_bf", z2_rows), halves)
+        b_ps = product("lo", w3_q, z2_q)
+
+        out_rows = out.rearrange("(p t) c -> p t c", t=PACK)
+        b_sb = [sb(f"b{t}", [P, S], F32) for t in planes]
+        b_at = [sb(f"b_at{t}", [P, S], F32) for t in planes]
+        sig_turned = [sb(f"sig_turned{t}", [P, S], F32) for t in planes]
+        res = [sb(f"res{t}", [P, S], F32) for t in planes]
+        blocks = [slice(P * u, P * (u + 1)) for u in range(S // P)]
+
+        def add_a(t):
+            nc.vector.tensor_tensor(out=a_sum[t][:], in0=a_ps[t][:], in1=a_at[t][:], op=ALU.add)
+
+        def finish(t, parts):
+            turned = psum.tile([P, S], F32, name=f"turned{t}", tag=f"lo{t}")
+            for cols in blocks:
+                nc.tensor.matmul(out=turned[:, cols], lhsT=b_sb[t][:, cols], rhs=ident[:], is_transpose=True, start=True, stop=False)
+                nc.tensor.matmul(out=turned[:, cols], lhsT=b_at[t][:, cols], rhs=ident[:], is_transpose=True, start=False, stop=True)
+            nc.scalar.activation(out=sig_turned[t][:], in_=turned[:], func=ACT.Sigmoid)
+            sig = psum.tile([P, S], F32, name=f"sig{t}", tag=f"hi{t}")
+            for cols in blocks:
+                nc.tensor.transpose(out=sig[:, cols], in_=sig_turned[t][:, cols], identity=ident[:])
+            for cols in parts:
+                nc.vector.tensor_tensor(out=res[t][:, cols], in0=sig[:, cols], in1=a_sum[t][:, cols], op=ALU.mult)
+                nc.sync.dma_start(out=out_rows[:, t, cols], in_=res[t][:, cols])
+
+        add_a(0)
+        for t in planes:
+            nc.scalar.copy(out=b_sb[t][:], in_=b_ps[t][:])
+        for t, h, engine in [(0, 0, nc.vector), (0, 1, nc.vector), (1, 0, nc.vector), (1, 1, nc.vector), (2, 0, nc.vector),
+                             (3, 0, nc.scalar), (3, 1, nc.scalar), (2, 1, nc.scalar)]:
+            gather(engine, b_at[t][:, halves[h]], b_sb[t], n7_sb, halves[h])
+        add_a(1)
+        finish(0, [slice(0, S)])
+        add_a(3)
+        finish(1, [slice(0, S)])
+        add_a(2)
+        finish(3, [slice(0, S)])
+        finish(2, halves)

@@ -32,8 +32,8 @@ def tile_picked_forktriebkindafold_none_p_kernel(
         keep = ctx.enter_context(tc.tile_pool(name="keep", bufs=1))
         psum = ctx.enter_context(tc.psum_pool(name="psum", bufs=1))
 
-        def sb(name, shape, dtype):
-            return keep.tile(shape, dtype, name=name, align_bytes=64)
+        def sb(name, shape, dtype, after=None):
+            return keep.tile(shape, dtype, name=name, tag=after or name, align_bytes=64)
 
         def load_list(name, src):
             tile = keep.tile(list(src.shape), U16, name=name)
@@ -113,24 +113,32 @@ def tile_picked_forktriebkindafold_none_p_kernel(
         make_identity(nc, ident[:])
 
         tab_rows = tab.rearrange("(p t) c -> p t c", t=PACK)
-        tab_sb = [sb(f"tab{t}", [P, S], F32) for t in planes]
-        n1_sb = load_list("n1_sb", n1)
-        nc.sync.dma_start(out=tab_sb[0][:], in_=tab_rows[:, 0, :])
-        n2_sb = load_list("n2_sb", n2)
-        nc.sync.dma_start(out=tab_sb[1][:], in_=tab_rows[:, 1, :])
-        for q in range(4):
+        warm = sb("warm", [P, 16], F32)
+        nc.vector.memset(warm[:, 0:1], 0.0)
+        nc.scalar.activation(out=warm[:, 8:9], in_=warm[:, 0:1], func=ACT.Sigmoid)
+        tab_win = [sb(f"tab{t}", [P, 2 * S], F32) for t in planes]
+        tab_sb = [w[:, S:] for w in tab_win]
+        def load_scale_rows(q):
             nc.sync.dma_start(
                 out=x_scale_rows[32 * q : 32 * q + 4, :].bitcast(I32),
                 in_=x_scales[0, 4 * q : 4 * q + 4, :].bitcast(I32),
             )
-        for t in range(2, PACK):
-            nc.sync.dma_start(out=tab_sb[t][:], in_=tab_rows[:, t, :])
+
+        nc.sync.dma_start(out=gn_sb[:], in_=gn.rearrange("(p t) o -> p (t o)", t=PACK))
+        nc.sync.dma_start(out=tab_sb[0], in_=tab_rows[:, 0, :])
+        n1_sb = load_list("n1_sb", n1)
+        n2_sb = load_list("n2_sb", n2)
+        nc.sync.dma_start(out=tab_sb[1], in_=tab_rows[:, 1, :])
+        nc.sync.dma_start(out=tab_sb[2], in_=tab_rows[:, 2, :])
         offs_sb = load_list("offs_sb", offs)
+        load_scale_rows(0)
         w1_raw = load_weight("w1", w1)
+        for q in range(1, 4):
+            load_scale_rows(q)
+        nc.sync.dma_start(out=tab_sb[3], in_=tab_rows[:, 3, :])
         x_word_rows = sb("x_word_rows", [P, T], I32)
         nc.sync.dma_start(out=x_word_rows[:], in_=x_words[0].rearrange("p n t -> p (n t)").bitcast(I32))
         n3_sb = load_list("n3_sb", n3)
-        nc.sync.dma_start(out=gn_sb[:], in_=gn.rearrange("(p t) o -> p (t o)", t=PACK))
         w2_raw = load_weight("w2", w2)
         n5_sb = load_list("n5_sb", n5)
         n4_sb = load_list("n4_sb", n4)
@@ -139,92 +147,92 @@ def tile_picked_forktriebkindafold_none_p_kernel(
         n6_sb = load_list("n6_sb", n6)
         n7_sb = load_list("n7_sb", n7)
 
-        factor = [sb(f"factor{t}", [P, S], F32) for t in planes]
-        shift = [sb(f"shift{t}", [P, S], F32) for t in planes]
+        last = PACK - 1
+        every = slice(0, S)
+        y_win = [sb(f"y{t}", [P, 2 * S], F32) for t in planes]
+        a_win = [sb(f"a{t}", [P, 2 * S], F32) for t in planes]
+        b_win = [sb(f"b{t}", [P, 2 * S], F32) for t in planes]
+        y_sb = [w[:, :S] for w in y_win]
+        a_sb = [w[:, :S] for w in a_win]
+        b_sb = [w[:, :S] for w in b_win]
+        factor = [w[:, S:] for w in y_win]
+        shift_rows = sb("shift_rows", [P, PACK, S], F32)
+        y_at = [w[:, S:] for w in b_win]
         for t in planes:
-            for cols in halves:
-                gather(nc.scalar, factor[t][:, cols], tab_sb[t], n1_sb, cols)
-            for cols in halves:
-                gather(nc.vector if t < 2 else nc.scalar, shift[t][:, cols], tab_sb[t], n2_sb, cols)
+            nc.vector.tensor_scalar(
+                out=tab_win[t][:, :S], in0=tab_sb[t], scalar1=gn_sb[:, t : t + 1], scalar2=None, op0=ALU.mult
+            )
+        for t in planes:
+            gather(nc.scalar, factor[t], tab_win[t], n1_sb, every)
+            gather(nc.vector if t < 2 else nc.scalar, shift_rows[:, t, :], tab_win[t], n2_sb, every)
 
         x_codes = sb("x_codes", [P, S], U32)
         x_scale = sb("x_scale", [P, S], U8)
+        w1_bf = deal_weight(nc.vector, "w1", w1_raw)
         nc.vector.tensor_copy(out=x_scale[:], in_=x_scale_rows[:].indirect(offs_sb[:]))
-        w1_q = quantize("w1", deal_weight(nc.vector, "w1", w1_raw), [slice(0, S)])
+        w1_q = quantize("w1", w1_bf, [every])
         nc.vector.tensor_copy(out=x_codes[:], in_=x_word_rows[:].bitcast(U32).indirect(offs_sb[:]))
         y_ps = product("lo", w1_q, (x_codes, x_scale))
 
-        y_sb = [sb(f"y{t}", [P, S], F32) for t in planes]
-        y_at = [sb(f"y_at{t}", [P, S], F32) for t in planes]
-        scaled = [sb(f"scaled{t}", [P, S], F32) for t in planes]
-        z_rows = sb("z_rows", [P, PACK, S], BF16)
-        w2_q = quantize("w2", deal_weight(nc.vector, "w2", w2_raw), [slice(0, S)])
 
         def scale_up(t, cols):
-            nc.vector.scalar_tensor_tensor(
-                out=scaled[t][:, cols], in0=y_at[t][:, cols], scalar=gn_sb[:, t : t + 1], in1=factor[t][:, cols],
-                op0=ALU.mult, op1=ALU.mult,
-            )
+            nc.vector.tensor_tensor(out=scaled[t][:, cols], in0=y_at[t][:, cols], in1=factor[t][:, cols], op=ALU.mult)
 
-        def add_shift(t, cols):
-            nc.vector.scalar_tensor_tensor(
-                out=z_rows[:, t, cols], in0=shift[t][:, cols], scalar=gn_sb[:, t : t + 1], in1=scaled[t][:, cols],
-                op0=ALU.mult, op1=ALU.add,
-            )
-
-        last = PACK - 1
-        every = slice(0, S)
-        nc.scalar.copy(out=y_sb[0][:], in_=y_ps[0][:])
+        copy(nc.vector, y_sb[0], y_ps[0][:])
+        w2_bf = deal_weight(nc.vector, "w2", w2_raw)
+        w2_q = quantize("w2", w2_bf, [every])
+        w3_q = quantize("w3", deal_weight(nc.vector, "w3", w3_raw), [every])
+        scaled_rows = sb("scaled_rows", [P, PACK, S], F32, after="w3_bf")
+        scaled = [scaled_rows[:, t, :] for t in planes]
         for t in planes:
             if t < last:
-                nc.scalar.copy(out=y_sb[t + 1][:], in_=y_ps[t + 1][:])
-            for cols in halves:
-                gather(nc.scalar, y_at[t][:, cols], y_sb[t], n3_sb, cols)
-            if t < last:
-                scale_up(t, every)
-            if t > 0:
-                add_shift(t - 1, every)
-            if t == 0:
-                w3_q = quantize("w3", deal_weight(nc.vector, "w3", w3_raw), [every])
+                copy(nc.scalar, y_sb[t + 1], y_ps[t + 1][:])
+            for cols in halves if t == last else [every]:
+                gather(nc.scalar, y_at[t][:, cols], y_win[t], n3_sb, cols)
+                scale_up(t, cols)
+        z_bf = sb("z_bf", [P, S * PACK], BF16)
         for cols in halves:
-            scale_up(last, cols)
-        for cols in halves:
-            add_shift(last, cols)
-        z_q = quantize("z", weave(nc.vector, "z_bf", z_rows), halves)
+            nc.vector.tensor_tensor(
+                out=z_bf[:, PACK * cols.start : PACK * cols.stop].rearrange("p (c i t) -> p c t i", i=4, t=PACK),
+                in0=scaled_rows[:, :, cols].rearrange("p t (c i) -> p c t i", i=4),
+                in1=shift_rows[:, :, cols].rearrange("p t (c i) -> p c t i", i=4),
+                op=ALU.add,
+            )
+        z_q = quantize("z", z_bf, halves)
         a_ps = product("hi", w2_q, z_q)
 
-        whole = slice(0, HALF)
-        gate = [sb(f"gate{t}", [P, HALF], F32) for t in planes]
-        kept = [sb(f"kept{t}", [P, HALF], F32) for t in planes]
+        pairs = slice(0, HALF)
+        gate = [w[:, S : S + HALF] for w in a_win]
+        kept = [w[:, S + HALF :] for w in a_win]
         z2_rows = sb("z2_rows", [P, PACK, S], BF16)
-        for t in planes:
-            gather(nc.scalar, gate[t][:], y_sb[t], n5_sb, whole, func=ACT.Sigmoid)
-            gather(nc.scalar, kept[t][:], y_sb[t], n4_sb, whole)
-        for t in planes:
-            nc.vector.tensor_tensor(out=y_sb[t][:].indirect(n5_sb[:]), in0=kept[t][:], in1=gate[t][:], op=ALU.mult)
-            if t > 0:
-                nc.vector.tensor_scalar(
-                    out=z2_rows[:, t - 1, :], in0=y_sb[t - 1][:], scalar1=gm_sb[:, t - 1 : t], scalar2=None, op0=ALU.mult
-                )
-
-        a_sb = [sb(f"a{t}", [P, S], F32) for t in planes]
         a_at = [sb(f"a_at{t}", [P, S], F32) for t in planes]
         a_sum = [sb(f"a_sum{t}", [P, S], F32) for t in planes]
-        nc.scalar.copy(out=a_sb[0][:], in_=a_ps[0][:])
+
+        def gain(engine, t, cols):
+            if engine is nc.vector:
+                nc.vector.tensor_scalar(
+                    out=z2_rows[:, t, cols], in0=y_sb[t][:, cols], scalar1=gm_sb[:, t : t + 1], scalar2=None, op0=ALU.mult
+                )
+            else:
+                nc.scalar.activation(out=z2_rows[:, t, cols], in_=y_sb[t][:, cols], func=ACT.Copy, scale=gm_sb[:, t : t + 1])
+
         for t in planes:
+            gather(nc.scalar, gate[t], y_win[t], n5_sb, pairs, func=ACT.Sigmoid)
+            gather(nc.scalar, kept[t], y_win[t], n4_sb, pairs)
+        copy(nc.scalar, a_sb[0], a_ps[0][:])
+        for t in planes:
+            nc.vector.tensor_tensor(out=y_win[t][:].indirect(n5_sb[:]), in0=kept[t], in1=gate[t], op=ALU.mult)
             if t < last:
-                nc.scalar.copy(out=a_sb[t + 1][:], in_=a_ps[t + 1][:])
-            for cols in halves:
-                gather(nc.scalar, a_at[t][:, cols], a_sb[t], n6_sb, cols)
+                copy(nc.scalar, a_sb[t + 1], a_ps[t + 1][:])
+            gather(nc.scalar, a_at[t][:], a_win[t], n6_sb, every)
+            if t > 0:
+                gain(nc.vector, t - 1, every)
         for cols in halves:
-            nc.vector.tensor_scalar(
-                out=z2_rows[:, last, cols], in0=y_sb[last][:, cols], scalar1=gm_sb[:, last:], scalar2=None, op0=ALU.mult
-            )
+            gain(nc.vector, last, cols)
         z2_q = quantize("z2", weave(nc.vector, "z2_bf", z2_rows), halves)
         b_ps = product("lo", w3_q, z2_q)
 
         out_rows = out.rearrange("(p t) c -> p t c", t=PACK)
-        b_sb = [sb(f"b{t}", [P, S], F32) for t in planes]
         b_at = [sb(f"b_at{t}", [P, S], F32) for t in planes]
         sig_turned = [sb(f"sig_turned{t}", [P, S], F32) for t in planes]
         res = [sb(f"res{t}", [P, S], F32) for t in planes]
@@ -233,11 +241,23 @@ def tile_picked_forktriebkindafold_none_p_kernel(
         def add_a(t):
             nc.vector.tensor_tensor(out=a_sum[t][:], in0=a_ps[t][:], in1=a_at[t][:], op=ALU.add)
 
-        def finish(t, parts):
-            turned = psum.tile([P, S], F32, name=f"turned{t}", tag=f"lo{t}")
+        turned_ps = {}
+
+        def turn_plain(t):
+            turned_ps[t] = psum.tile([P, S], F32, name=f"turned{t}", tag=f"lo{t}")
             for cols in blocks:
-                nc.tensor.matmul(out=turned[:, cols], lhsT=b_sb[t][:, cols], rhs=ident[:], is_transpose=True, start=True, stop=False)
-                nc.tensor.matmul(out=turned[:, cols], lhsT=b_at[t][:, cols], rhs=ident[:], is_transpose=True, start=False, stop=True)
+                nc.tensor.matmul(
+                    out=turned_ps[t][:, cols], lhsT=b_sb[t][:, cols], rhs=ident[:], is_transpose=True,
+                    start=cols.start == 0, stop=False,
+                )
+
+        def finish(t, parts):
+            turned = turned_ps[t]
+            for cols in blocks:
+                nc.tensor.matmul(
+                    out=turned[:, cols], lhsT=b_at[t][:, cols], rhs=ident[:], is_transpose=True,
+                    start=False, stop=cols.stop == S,
+                )
             nc.scalar.activation(out=sig_turned[t][:], in_=turned[:], func=ACT.Sigmoid)
             sig = psum.tile([P, S], F32, name=f"sig{t}", tag=f"hi{t}")
             for cols in blocks:
@@ -246,16 +266,30 @@ def tile_picked_forktriebkindafold_none_p_kernel(
                 nc.vector.tensor_tensor(out=res[t][:, cols], in0=sig[:, cols], in1=a_sum[t][:, cols], op=ALU.mult)
                 nc.sync.dma_start(out=out_rows[:, t, cols], in_=res[t][:, cols])
 
+        def finish_direct(t, parts):
+            for cols in parts:
+                nc.vector.tensor_tensor(out=b_sum[t][:, cols], in0=b_ps[t][:, cols], in1=b_at[t][:, cols], op=ALU.add)
+            for cols in parts:
+                nc.scalar.activation(out=sig_turned[t][:, cols], in_=b_sum[t][:, cols], func=ACT.Sigmoid)
+            for cols in parts:
+                nc.vector.tensor_tensor(out=res[t][:, cols], in0=sig_turned[t][:, cols], in1=a_sum[t][:, cols], op=ALU.mult)
+                nc.sync.dma_start(out=out_rows[:, t, cols], in_=res[t][:, cols])
+
+        b_sum = [sb(f"b_sum{t}", [P, S], F32) for t in planes]
         add_a(0)
         for t in planes:
-            nc.scalar.copy(out=b_sb[t][:], in_=b_ps[t][:])
-        for t, h, engine in [(0, 0, nc.vector), (0, 1, nc.vector), (1, 0, nc.vector), (1, 1, nc.vector), (2, 0, nc.vector),
-                             (3, 0, nc.scalar), (3, 1, nc.scalar), (2, 1, nc.scalar)]:
-            gather(engine, b_at[t][:, halves[h]], b_sb[t], n7_sb, halves[h])
+            copy(nc.scalar, b_sb[t], b_ps[t][:])
+            if t < 2:
+                turn_plain(t)
+        for t in range(2):
+            gather(nc.vector, b_at[t][:], b_win[t], n7_sb, every)
+        gather(nc.scalar, b_at[2][:], b_win[2], n7_sb, every)
         add_a(1)
-        finish(0, [slice(0, S)])
-        add_a(3)
-        finish(1, [slice(0, S)])
         add_a(2)
-        finish(3, [slice(0, S)])
-        finish(2, halves)
+        finish(0, [every])
+        add_a(last)
+        for cols in halves:
+            gather(nc.scalar, b_at[last][:, cols], b_win[last], n7_sb, cols)
+        finish(1, [every])
+        finish_direct(2, [every])
+        finish_direct(last, halves)

from contextlib import ExitStack

import concourse.mybir as mybir
from concourse.masks import make_identity

K, T, S, N, H = 512, 2048, 512, 512, 512
FLOPS = 3 * 2 * 512 * 512 * 512

F32 = mybir.dt.float32
BF16 = mybir.dt.bfloat16
I32 = mybir.dt.int32
U32 = mybir.dt.uint32
U16 = mybir.dt.uint16
U8 = mybir.dt.uint8
FP8X4 = mybir.dt.float8_e4m3fn_x4
ACT = mybir.ActivationFunctionType
ALU = mybir.AluOpType

P = 128
PACK = 4
HALF = S // 2


def tile_picked_forktriebkindafold_none_p_kernel(
    tc, x_words, x_scales, w1, tab, gn, w2, gm, w3, offs, n1, n2, n3, n4, n5, n6, n7, out
):
    nc = tc.nc
    planes = range(PACK)
    halves = [slice(0, HALF), slice(HALF, S)]

    with ExitStack() as ctx:
        keep = ctx.enter_context(tc.tile_pool(name="keep", bufs=1))
        psum = ctx.enter_context(tc.psum_pool(name="psum", bufs=1))

        def sb(name, shape, dtype, after=None):
            return keep.tile(shape, dtype, name=name, tag=after or name, align_bytes=64)

        def load_list(name, src):
            tile = keep.tile(list(src.shape), U16, name=name)
            nc.sync.dma_start(tile[:], src)
            return tile

        def load_weight(name, w):
            raw = sb(name + "_raw", [P, PACK, N], F32)
            nc.sync.dma_start(out=raw[:], in_=w.rearrange("(p j) c -> p j c", j=PACK))
            return raw

        def gather(engine, dst, window, lst, cols, func=ACT.Copy):
            picked = window[:].indirect(lst[:, cols.start // 16 : cols.stop // 16])
            if engine is nc.vector:
                nc.vector.tensor_copy(out=dst, in_=picked)
            else:
                nc.scalar.activation(out=dst, in_=picked, func=func)

        def copy(engine, dst, src):
            if engine is nc.vector:
                nc.vector.tensor_copy(out=dst, in_=src)
            else:
                nc.scalar.copy(out=dst, in_=src)

        def deal_weight(engine, name, raw):
            dealt = sb(name + "_bf", [P, N * PACK], BF16)
            copy(
                engine,
                dealt[:].rearrange("p (t m j) -> p m j t", t=PACK, j=PACK),
                raw[:].rearrange("p j (m t) -> p m j t", t=PACK),
            )
            return dealt

        def quantize(name, values, parts):
            codes = sb(name + "_codes", [P, S], U32)
            scales = sb(name + "_scales", [P, S], U8)
            for cols in parts:
                nc.vector.quantize_mx(
                    out=codes[:, cols].bitcast(FP8X4),
                    scales=scales[:, cols],
                    in_=values[:, PACK * cols.start : PACK * cols.stop],
                )
            return codes, scales

        def weave(engine, name, rows):
            woven = sb(name, [P, S * PACK], BF16)
            for cols in halves:
                copy(
                    engine,
                    woven[:, PACK * cols.start : PACK * cols.stop].rearrange("p (c i t) -> p c t i", i=4, t=PACK),
                    rows[:, :, cols].rearrange("p t (c i) -> p c t i", i=4),
                )
            return woven

        def product(tag, weight, moving):
            banks = []
            for t in planes:
                bank = psum.tile([P, S], F32, name=f"{tag}{t}", tag=f"{tag}{t}")
                m_cols = slice(P * t, P * (t + 1))
                nc.tensor.matmul_mx(
                    out=bank[:],
                    lhsT=weight[0][:, m_cols].bitcast(FP8X4),
                    lhsT_scale=weight[1][:, m_cols],
                    rhs=moving[0][:].bitcast(FP8X4),
                    rhs_scale=moving[1][:],
                    start=True,
                    stop=True,
                )
                banks.append(bank)
            return banks

        x_scale_rows = sb("x_scale_rows", [P, T], U8)
        nc.vector.memset(x_scale_rows[:].bitcast(I32), 0)
        gn_sb = sb("gn_sb", [P, PACK], F32)
        gm_sb = sb("gm_sb", [P, PACK], F32)
        ident = sb("ident", [P, P], F32)
        make_identity(nc, ident[:])

        tab_rows = tab.rearrange("(p t) c -> p t c", t=PACK)
        warm = sb("warm", [P, 16], F32)
        nc.vector.memset(warm[:, 0:1], 0.0)
        nc.scalar.activation(out=warm[:, 8:9], in_=warm[:, 0:1], func=ACT.Sigmoid)
        tab_win = [sb(f"tab{t}", [P, 2 * S], F32) for t in planes]
        tab_sb = [w[:, S:] for w in tab_win]
        def load_scale_rows(q):
            nc.sync.dma_start(
                out=x_scale_rows[32 * q : 32 * q + 4, :].bitcast(I32),
                in_=x_scales[0, 4 * q : 4 * q + 4, :].bitcast(I32),
            )

        nc.sync.dma_start(out=gn_sb[:], in_=gn.rearrange("(p t) o -> p (t o)", t=PACK))
        nc.sync.dma_start(out=tab_sb[0], in_=tab_rows[:, 0, :])
        n1_sb = load_list("n1_sb", n1)
        n2_sb = load_list("n2_sb", n2)
        nc.sync.dma_start(out=tab_sb[1], in_=tab_rows[:, 1, :])
        nc.sync.dma_start(out=tab_sb[2], in_=tab_rows[:, 2, :])
        offs_sb = load_list("offs_sb", offs)
        load_scale_rows(0)
        w1_raw = load_weight("w1", w1)
        for q in range(1, 4):
            load_scale_rows(q)
        nc.sync.dma_start(out=tab_sb[3], in_=tab_rows[:, 3, :])
        x_word_rows = sb("x_word_rows", [P, T], I32)
        nc.sync.dma_start(out=x_word_rows[:], in_=x_words[0].rearrange("p n t -> p (n t)").bitcast(I32))
        n3_sb = load_list("n3_sb", n3)
        w2_raw = load_weight("w2", w2)
        n5_sb = load_list("n5_sb", n5)
        n4_sb = load_list("n4_sb", n4)
        w3_raw = load_weight("w3", w3)
        nc.sync.dma_start(out=gm_sb[:], in_=gm.rearrange("(p t) o -> p (t o)", t=PACK))
        n6_sb = load_list("n6_sb", n6)
        n7_sb = load_list("n7_sb", n7)

        last = PACK - 1
        every = slice(0, S)
        y_win = [sb(f"y{t}", [P, 2 * S], F32) for t in planes]
        a_win = [sb(f"a{t}", [P, 2 * S], F32) for t in planes]
        b_win = [sb(f"b{t}", [P, 2 * S], F32) for t in planes]
        y_sb = [w[:, :S] for w in y_win]
        a_sb = [w[:, :S] for w in a_win]
        b_sb = [w[:, :S] for w in b_win]
        factor = [w[:, S:] for w in y_win]
        shift_rows = sb("shift_rows", [P, PACK, S], F32)
        y_at = [w[:, S:] for w in b_win]
        for t in planes:
            nc.vector.tensor_scalar(
                out=tab_win[t][:, :S], in0=tab_sb[t], scalar1=gn_sb[:, t : t + 1], scalar2=None, op0=ALU.mult
            )
        for t in planes:
            gather(nc.scalar, factor[t], tab_win[t], n1_sb, every)
            gather(nc.vector if t < 2 else nc.scalar, shift_rows[:, t, :], tab_win[t], n2_sb, every)

        x_codes = sb("x_codes", [P, S], U32)
        x_scale = sb("x_scale", [P, S], U8)
        w1_bf = deal_weight(nc.vector, "w1", w1_raw)
        nc.vector.tensor_copy(out=x_scale[:], in_=x_scale_rows[:].indirect(offs_sb[:]))
        w1_q = quantize("w1", w1_bf, [every])
        nc.vector.tensor_copy(out=x_codes[:], in_=x_word_rows[:].bitcast(U32).indirect(offs_sb[:]))
        y_ps = product("lo", w1_q, (x_codes, x_scale))


        def scale_up(t, cols):
            nc.vector.tensor_tensor(out=scaled[t][:, cols], in0=y_at[t][:, cols], in1=factor[t][:, cols], op=ALU.mult)

        copy(nc.vector, y_sb[0], y_ps[0][:])
        w2_bf = deal_weight(nc.vector, "w2", w2_raw)
        w2_q = quantize("w2", w2_bf, [every])
        w3_q = quantize("w3", deal_weight(nc.vector, "w3", w3_raw), [every])
        scaled_rows = sb("scaled_rows", [P, PACK, S], F32, after="w3_bf")
        scaled = [scaled_rows[:, t, :] for t in planes]
        for t in planes:
            if t < last:
                copy(nc.scalar, y_sb[t + 1], y_ps[t + 1][:])
            for cols in halves if t == last else [every]:
                gather(nc.scalar, y_at[t][:, cols], y_win[t], n3_sb, cols)
                scale_up(t, cols)
        z_bf = sb("z_bf", [P, S * PACK], BF16)
        for cols in halves:
            nc.vector.tensor_tensor(
                out=z_bf[:, PACK * cols.start : PACK * cols.stop].rearrange("p (c i t) -> p c t i", i=4, t=PACK),
                in0=scaled_rows[:, :, cols].rearrange("p t (c i) -> p c t i", i=4),
                in1=shift_rows[:, :, cols].rearrange("p t (c i) -> p c t i", i=4),
                op=ALU.add,
            )
        z_q = quantize("z", z_bf, halves)
        a_ps = product("hi", w2_q, z_q)

        pairs = slice(0, HALF)
        gate = [w[:, S : S + HALF] for w in a_win]
        kept = [w[:, S + HALF :] for w in a_win]
        z2_rows = sb("z2_rows", [P, PACK, S], BF16)
        a_at = [sb(f"a_at{t}", [P, S], F32) for t in planes]
        a_sum = [sb(f"a_sum{t}", [P, S], F32) for t in planes]

        def gain(engine, t, cols):
            if engine is nc.vector:
                nc.vector.tensor_scalar(
                    out=z2_rows[:, t, cols], in0=y_sb[t][:, cols], scalar1=gm_sb[:, t : t + 1], scalar2=None, op0=ALU.mult
                )
            else:
                nc.scalar.activation(out=z2_rows[:, t, cols], in_=y_sb[t][:, cols], func=ACT.Copy, scale=gm_sb[:, t : t + 1])

        for t in planes:
            gather(nc.scalar, gate[t], y_win[t], n5_sb, pairs, func=ACT.Sigmoid)
            gather(nc.scalar, kept[t], y_win[t], n4_sb, pairs)
        copy(nc.scalar, a_sb[0], a_ps[0][:])
        for t in planes:
            nc.vector.tensor_tensor(out=y_win[t][:].indirect(n5_sb[:]), in0=kept[t], in1=gate[t], op=ALU.mult)
            if t < last:
                copy(nc.scalar, a_sb[t + 1], a_ps[t + 1][:])
            gather(nc.scalar, a_at[t][:], a_win[t], n6_sb, every)
            if t > 0:
                gain(nc.vector, t - 1, every)
        for cols in halves:
            gain(nc.vector, last, cols)
        z2_q = quantize("z2", weave(nc.vector, "z2_bf", z2_rows), halves)
        b_ps = product("lo", w3_q, z2_q)

        out_rows = out.rearrange("(p t) c -> p t c", t=PACK)
        b_at = [sb(f"b_at{t}", [P, S], F32) for t in planes]
        sig_turned = [sb(f"sig_turned{t}", [P, S], F32) for t in planes]
        res = [sb(f"res{t}", [P, S], F32) for t in planes]
        blocks = [slice(P * u, P * (u + 1)) for u in range(S // P)]

        def add_a(t):
            nc.vector.tensor_tensor(out=a_sum[t][:], in0=a_ps[t][:], in1=a_at[t][:], op=ALU.add)

        turned_ps = {}

        def turn_plain(t):
            turned_ps[t] = psum.tile([P, S], F32, name=f"turned{t}", tag=f"lo{t}")
            for cols in blocks:
                nc.tensor.matmul(
                    out=turned_ps[t][:, cols], lhsT=b_sb[t][:, cols], rhs=ident[:], is_transpose=True,
                    start=cols.start == 0, stop=False,
                )

        def finish(t, parts):
            turned = turned_ps[t]
            for cols in blocks:
                nc.tensor.matmul(
                    out=turned[:, cols], lhsT=b_at[t][:, cols], rhs=ident[:], is_transpose=True,
                    start=False, stop=cols.stop == S,
                )
            nc.scalar.activation(out=sig_turned[t][:], in_=turned[:], func=ACT.Sigmoid)
            sig = psum.tile([P, S], F32, name=f"sig{t}", tag=f"hi{t}")
            for cols in blocks:
                nc.tensor.transpose(out=sig[:, cols], in_=sig_turned[t][:, cols], identity=ident[:])
            for cols in parts:
                nc.vector.tensor_tensor(out=res[t][:, cols], in0=sig[:, cols], in1=a_sum[t][:, cols], op=ALU.mult)
                nc.sync.dma_start(out=out_rows[:, t, cols], in_=res[t][:, cols])

        def finish_direct(t, parts):
            for cols in parts:
                nc.vector.tensor_tensor(out=b_sum[t][:, cols], in0=b_ps[t][:, cols], in1=b_at[t][:, cols], op=ALU.add)
            for cols in parts:
                nc.scalar.activation(out=sig_turned[t][:, cols], in_=b_sum[t][:, cols], func=ACT.Sigmoid)
            for cols in parts:
                nc.vector.tensor_tensor(out=res[t][:, cols], in0=sig_turned[t][:, cols], in1=a_sum[t][:, cols], op=ALU.mult)
                nc.sync.dma_start(out=out_rows[:, t, cols], in_=res[t][:, cols])

        b_sum = [sb(f"b_sum{t}", [P, S], F32) for t in planes]
        add_a(0)
        for t in planes:
            copy(nc.scalar, b_sb[t], b_ps[t][:])
            if t < 2:
                turn_plain(t)
        for t in range(2):
            gather(nc.vector, b_at[t][:], b_win[t], n7_sb, every)
        gather(nc.scalar, b_at[2][:], b_win[2], n7_sb, every)
        add_a(1)
        add_a(2)
        finish(0, [every])
        add_a(last)
        for cols in halves:
            gather(nc.scalar, b_at[last][:, cols], b_win[last], n7_sb, cols)
        finish(1, [every])
        finish_direct(2, [every])
        finish_direct(last, halves)
